import numpy as np
import ml_dtypes


def mxq(x, axis, fmt="e4m3"):
    dtype, down = {"e4m3": (ml_dtypes.float8_e4m3fn, 7), "e5m2": (ml_dtypes.float8_e5m2, 14)}[fmt]
    v = np.moveaxis(np.asarray(x, np.float32).astype(ml_dtypes.bfloat16).astype(np.float64), axis, -1)
    blocks = v.reshape(v.shape[:-1] + (-1, 32))
    amax = np.abs(blocks).max(-1, keepdims=True)
    byte = np.maximum(np.where(amax > 0, np.frexp(amax)[1] - 1 + 127, 0) - down, 1)
    scale = np.exp2(byte - 127.0)
    codes = (blocks / scale).astype(np.float32).astype(dtype).astype(np.float64)
    return np.moveaxis((codes * scale).reshape(v.shape), -1, axis)


WIDE = False


def mx_kscale(k):
    if not WIDE:
        return np.ones(k)
    levels = np.array([10, -10, 5, -5, 0])
    if k % 512:
        return np.exp2(np.random.permutation(np.resize(levels, k // 32))).repeat(32)
    a = np.empty((k // 512, 16))
    for p in range(k // 512):
        a[p, :8] = np.random.permutation(np.resize(levels, 8))
        for g in range(8):
            far = levels[np.abs(levels - a[p, g]) >= 10]
            a[p, g + 8] = far[np.random.randint(len(far))]
    return np.exp2(a.ravel()).repeat(32)


def f64(x):
    return np.asarray(x).astype(np.float64)


def striped8(idx):
    return np.asarray(idx).reshape(8, -1, 16).transpose(0, 2, 1).reshape(128, -1).astype(np.uint16)


def unstriped8(offs):
    return offs.reshape(8, 16, -1).transpose(0, 2, 1).reshape(8, -1).astype(np.int64)


def pick8(x, idx, run):
    r = np.arange(len(x))
    return x[r[:, None], idx[r % (8 * run) // run]]


E2M1 = np.array([0.0, 0.5, 1.0, 1.5, 2.0, 3.0, 4.0, 6.0, -0.0, -0.5, -1.0, -1.5, -2.0, -3.0, -4.0, -6.0])


def pack_weight(w, fmt):
    k, n = w.shape
    w = f64(np.asarray(w, np.float32).astype(ml_dtypes.bfloat16)).reshape(k // 32, 32, n)
    amax = np.abs(w).max(1)
    if fmt == "e4m3":
        byte = np.frexp(amax)[1] - 1 + 127 - 7
    else:
        mant, ex = np.frexp(amax / 6.0)
        byte = np.where(mant > 0.5, ex, ex - 1) + 127
    byte = np.clip(np.where(amax > 0, byte, 1), 1, 254)
    scaled = (w * np.exp2(127.0 - byte)[:, None, :]).reshape(k, n).astype(np.float32)
    by_word = np.ascontiguousarray(scaled.reshape(k // 512, 128, 4, n).transpose(0, 1, 3, 2))
    if fmt == "e4m3":
        words = by_word.astype(ml_dtypes.float8_e4m3fn).view(np.uint8)
    else:
        c = by_word.astype(ml_dtypes.float4_e2m1fn).view(np.uint8) & 0xF
        words = (c[..., 0::2] | (c[..., 1::2] << 4)).reshape(k // 512, 128, 2 * n)
    return np.ascontiguousarray(words), np.ascontiguousarray(byte.astype(np.uint8).reshape(k // 512, 16, n))


def unpack_weight(words, scales, fmt):
    g, _, n = scales.shape
    words = np.ascontiguousarray(words).reshape(g, 128, n, -1)
    if fmt == "e4m3":
        vals = words.view(ml_dtypes.float8_e4m3fn).astype(np.float64)
    else:
        nib = np.empty((g, 128, n, 4), np.uint8)
        nib[..., 0::2] = words & 0xF
        nib[..., 1::2] = words >> 4
        vals = E2M1[nib]
    vals = vals * np.repeat(np.exp2(scales.astype(np.float64) - 127.0), 8, axis=1)[..., None]
    return vals.transpose(0, 1, 3, 2).reshape(g * 512, n)


D, T, I, Q = 512, 1024, 512, 128


def setup_inputs():
    n = np.random.standard_normal
    idx = np.stack([np.random.permutation(T)[:I] for _ in range(8)])
    idx2 = np.stack([np.random.permutation(T)[:I] for _ in range(8)])
    idx3 = np.stack([np.random.permutation(T)[:I] for _ in range(8)])
    idx4 = np.stack([np.random.permutation(T)[:I] for _ in range(8)])
    fd = mx_kscale(D)
    keysp = pack_weight(n((D, T)) / fd[:, None], "e2m1")
    return {
        "query": (n((D, Q)) * 1.0 / np.sqrt(D) * fd[:, None]).astype(np.float32),
        "keys_words": keysp[0],
        "keys_scales": keysp[1],
        "old": (np.random.uniform(0.3, 1.7, (Q, T))).astype(np.float32),
        "base": (0.5 * n((Q, T))).astype(np.float32),
        "offs": striped8(idx),
        "offs2": striped8(idx2),
        "offs3": striped8(idx3),
        "offs4": striped8(idx4),
    }


def reference(query, keys_words, keys_scales, old, base, offs, offs2, offs3, offs4):
    idx = unstriped8(offs)
    idx2 = unstriped8(offs2)
    idx3 = unstriped8(offs3)
    idx4 = unstriped8(offs4)
    keysu = unpack_weight(keys_words, keys_scales, "e2m1")
    queryq = mxq(f64(query), 0, "e4m3")
    a = queryq.T @ keysu
    s = pick8(a, idx, 16) - pick8(a, idx2, 16)
    w = np.maximum(s, 0.0)
    ws = w * pick8(f64(old), idx3, 16)
    f1 = np.zeros((Q, T))
    f1[np.arange(Q)[:, None], idx4[np.arange(Q) % 128 // 16]] = ws
    y = f64(base) + f1
    return y

from contextlib import ExitStack

import concourse.mybir as mybir

D, T, I, Q = 512, 1024, 512, 128
FLOPS = 2 * D * T * Q

F32 = mybir.dt.float32
BF16 = mybir.dt.bfloat16
I32 = mybir.dt.int32
U32 = mybir.dt.uint32
U16 = mybir.dt.uint16
U8 = mybir.dt.uint8
FP8X4 = mybir.dt.float8_e4m3fn_x4
FP4X4 = mybir.dt.float4_e2m1fn_x4
ALU = mybir.AluOpType
ACT = mybir.ActivationFunctionType

P = 128
PACK = 4
N_MM = 256
HALF = I // 2
QUARTER = I // 4
N_OUT = 256


def tile_attend_difference_lean_timesold_heads_kernel(
    tc, query, keys_words, keys_scales, old, base, offs, offs2, offs3, offs4, out
):
    nc = tc.nc
    with ExitStack() as ctx:
        pool = ctx.enter_context(tc.tile_pool(name="held", bufs=1))
        psum = ctx.enter_context(tc.psum_pool(name="psum", bufs=1))

        list1 = pool.tile([P, I // 16], U16, name="list1")
        list2 = pool.tile([P, I // 16], U16, name="list2")
        list3 = pool.tile([P, I // 16], U16, name="list3")
        list4 = pool.tile([P, I // 16], U16, name="list4")
        q_raw = pool.tile([P, PACK, Q], F32, name="q_raw")
        k_words = pool.tile([P, 2 * T], U8, name="k_words", align_bytes=64)
        k_scales = pool.tile([P, T], U8, name="k_scales", align_bytes=64)
        old_sb = pool.tile([P, T], F32, name="old_sb")
        base_sb = pool.tile([P, T], F32, name="base_sb")
        placed = pool.tile([P, T], F32, name="placed")
        scores = pool.tile([P, T], F32, name="scores")

        nc.vector.memset(k_scales[:].bitcast(I32), 0)
        nc.vector.memset(placed[:], 0.0)

        nc.sync.dma_start(out=q_raw[:], in_=query.rearrange("(p j) q -> p j q", j=PACK))
        nc.sync.dma_start(out=k_words[:].bitcast(I32), in_=keys_words[0].bitcast(I32))
        for quad in range(4):
            nc.sync.dma_start(
                out=k_scales[32 * quad : 32 * quad + 4, :].bitcast(I32),
                in_=keys_scales[0, 4 * quad : 4 * quad + 4, :].bitcast(I32),
            )
        nc.sync.dma_start(list3[:], offs3)
        nc.sync.dma_start(out=old_sb[:], in_=old)
        nc.sync.dma_start(list1[:], offs)
        nc.sync.dma_start(list2[:], offs2)
        nc.sync.dma_start(list4[:], offs4)
        nc.sync.dma_start(out=base_sb[:], in_=base)

        q_grouped = pool.tile([P, Q, PACK], BF16, name="q_grouped", align_bytes=64)
        q_codes = pool.tile([P, Q], U32, name="q_codes", align_bytes=64)
        q_scales = pool.tile([P, Q], U8, name="q_scales", align_bytes=64)
        q_halves = [slice(0, Q // 2), slice(Q // 2, Q)]
        for cols in q_halves:
            nc.vector.tensor_copy(out=q_grouped[:, cols, :], in_=q_raw[:, :, cols].rearrange("p j q -> p q j"))
        for cols in q_halves:
            nc.vector.quantize_mx(
                out=q_codes[:, cols].bitcast(FP8X4),
                scales=q_scales[:, cols],
                in_=q_grouped[:, cols, :].rearrange("p q j -> p (q j)"),
            )

        def slots(lst, start, count):
            return lst[:, start // 16 : (start + count) // 16]

        old_g0 = pool.tile([P, HALF], F32, name="old_g0")
        first = [pool.tile([P, HALF], F32, name=f"first{h}") for h in range(2)]
        second = [pool.tile([P, HALF], F32, name=f"second{h}") for h in range(2)]
        work = pool.tile([P, HALF], F32, name="work")
        diff0 = pool.tile([P, HALF], F32, name="diff0")
        pos1 = pool.tile([P, HALF], F32, name="pos1")
        diff = [diff0[:], diff0[:]]
        pos = [work[:, :HALF], pos1[:]]
        old_g = [old_g0, first[0]]

        n0 = 0
        for width in (256, 256, 128, 128, 128, 128):
            acc = psum.tile([P, width], F32, name=f"acc{n0}")
            nc.tensor.matmul_mx(
                out=acc[:],
                lhsT=q_codes[:].bitcast(FP8X4),
                lhsT_scale=q_scales[:],
                rhs=k_words[:, 2 * n0 : 2 * (n0 + width)].bitcast(FP4X4),
                rhs_scale=k_scales[:, n0 : n0 + width],
                start=True,
                stop=True,
            )
            if n0 < T // 2:
                nc.vector.tensor_copy(out=scores[:, n0 : n0 + width], in_=acc[:])
            else:
                nc.scalar.activation(scores[:, n0 : n0 + width], acc[:], ACT.Copy)
            n0 = n0 + width

        nc.vector.tensor_copy(old_g[0][:], old_sb[:].indirect(slots(list3, 0, HALF)))

        nc.scalar.activation(first[0][:], scores[:].indirect(slots(list1, 0, HALF)), ACT.Copy)
        nc.vector.tensor_copy(second[0][:], scores[:].indirect(slots(list2, 0, HALF)))
        nc.scalar.activation(first[1][:], scores[:].indirect(slots(list1, HALF, HALF)), ACT.Copy)
        nc.scalar.activation(second[1][:], scores[:].indirect(slots(list2, HALF, HALF)), ACT.Copy)

        def scatter(h, c0, count):
            nc.vector.tensor_tensor(
                placed[:].indirect(slots(list4, h * HALF + c0, count)),
                pos[h][:, c0 : c0 + count],
                old_g[h][:, c0 : c0 + count],
                ALU.mult,
            )

        quarters = [slice(QUARTER, HALF), slice(0, QUARTER)]
        for cols in quarters:
            nc.vector.tensor_tensor(diff0[:, cols], first[0][:, cols], second[0][:, cols], ALU.subtract)
        nc.scalar.activation(old_g[1][:], old_sb[:].indirect(slots(list3, HALF, HALF)), ACT.Copy)
        for cols in quarters:
            nc.vector.tensor_scalar_max(work[:, cols], diff0[:, cols], 0.0)

        scatter(0, QUARTER, QUARTER)
        nc.vector.tensor_tensor(diff[1], first[1][:], second[1][:], ALU.subtract)
        nc.scalar.activation(pos[1], diff[1], ACT.Relu)
        scatter(0, 0, QUARTER)
        scatter(1, 0, HALF)

        c0 = 0
        for i, width in enumerate((256, 256, 256, 128, 128)):
            res = pool.tile([P, width], F32, name=f"res{c0}")
            nc.vector.tensor_tensor(res[:], placed[:, c0 : c0 + width], base_sb[:, c0 : c0 + width], ALU.add)
            queue = nc.sync if i % 2 == 0 else nc.scalar
            queue.dma_start(out=out[:, c0 : c0 + width], in_=res[:])
            c0 = c0 + width
